import numpy as np
import ml_dtypes


def mxq(x, axis, fmt="e4m3"):
    dtype, down = {"e4m3": (ml_dtypes.float8_e4m3fn, 7), "e5m2": (ml_dtypes.float8_e5m2, 14)}[fmt]
    v = np.moveaxis(np.asarray(x, np.float32).astype(ml_dtypes.bfloat16).astype(np.float64), axis, -1)
    blocks = v.reshape(v.shape[:-1] + (-1, 32))
    amax = np.abs(blocks).max(-1, keepdims=True)
    byte = np.maximum(np.where(amax > 0, np.frexp(amax)[1] - 1 + 127, 0) - down, 1)
    scale = np.exp2(byte - 127.0)
    codes = (blocks / scale).astype(np.float32).astype(dtype).astype(np.float64)
    return np.moveaxis((codes * scale).reshape(v.shape), -1, axis)


WIDE = False


def mx_kscale(k):
    if not WIDE:
        return np.ones(k)
    levels = np.array([10, -10, 5, -5, 0])
    if k % 512:
        return np.exp2(np.random.permutation(np.resize(levels, k // 32))).repeat(32)
    a = np.empty((k // 512, 16))
    for p in range(k // 512):
        a[p, :8] = np.random.permutation(np.resize(levels, 8))
        for g in range(8):
            far = levels[np.abs(levels - a[p, g]) >= 10]
            a[p, g + 8] = far[np.random.randint(len(far))]
    return np.exp2(a.ravel()).repeat(32)


def f64(x):
    return np.asarray(x).astype(np.float64)


def striped(idx):
    return np.tile(np.asarray(idx).reshape(-1, 16).T, (8, 1)).astype(np.uint16)


def unstriped(offs):
    return offs[:16].T.reshape(-1).astype(np.int64)


E2M1 = np.array([0.0, 0.5, 1.0, 1.5, 2.0, 3.0, 4.0, 6.0, -0.0, -0.5, -1.0, -1.5, -2.0, -3.0, -4.0, -6.0])


def pack_weight(w, fmt):
    k, n = w.shape
    w = f64(np.asarray(w, np.float32).astype(ml_dtypes.bfloat16)).reshape(k // 32, 32, n)
    amax = np.abs(w).max(1)
    if fmt == "e4m3":
        byte = np.frexp(amax)[1] - 1 + 127 - 7
    else:
        mant, ex = np.frexp(amax / 6.0)
        byte = np.where(mant > 0.5, ex, ex - 1) + 127
    byte = np.clip(np.where(amax > 0, byte, 1), 1, 254)
    scaled = (w * np.exp2(127.0 - byte)[:, None, :]).reshape(k, n).astype(np.float32)
    by_word = np.ascontiguousarray(scaled.reshape(k // 512, 128, 4, n).transpose(0, 1, 3, 2))
    if fmt == "e4m3":
        words = by_word.astype(ml_dtypes.float8_e4m3fn).view(np.uint8)
    else:
        c = by_word.astype(ml_dtypes.float4_e2m1fn).view(np.uint8) & 0xF
        words = (c[..., 0::2] | (c[..., 1::2] << 4)).reshape(k // 512, 128, 2 * n)
    return np.ascontiguousarray(words), np.ascontiguousarray(byte.astype(np.uint8).reshape(k // 512, 16, n))


def unpack_weight(words, scales, fmt):
    g, _, n = scales.shape
    words = np.ascontiguousarray(words).reshape(g, 128, n, -1)
    if fmt == "e4m3":
        vals = words.view(ml_dtypes.float8_e4m3fn).astype(np.float64)
    else:
        nib = np.empty((g, 128, n, 4), np.uint8)
        nib[..., 0::2] = words & 0xF
        nib[..., 1::2] = words >> 4
        vals = E2M1[nib]
    vals = vals * np.repeat(np.exp2(scales.astype(np.float64) - 127.0), 8, axis=1)[..., None]
    return vals.transpose(0, 1, 3, 2).reshape(g * 512, n)


def sgn(shape):
    return np.random.uniform(0.5, 2.0, shape) * np.where(np.random.standard_normal(shape) < 0, -1.0, 1.0)


K, T, J, R, C, O, N = 512, 1024, 256, 512, 512, 256, 256


def setup_inputs():
    n = np.random.standard_normal
    idx = np.random.permutation(T)[:J]
    idx2 = np.random.permutation(C)[:J]
    idx3 = np.random.permutation(C)[:C]
    idx4 = np.random.permutation(C)[:O]
    fk = mx_kscale(K)
    fr = mx_kscale(R)
    xtp = pack_weight(n((K, T)) / fk[:, None], "e4m3")
    wp = pack_weight(n((K, R)) * 1 / np.sqrt(K) * fk[:, None], "e2m1")
    wbp = pack_weight(n((R, N)) * 1 / np.sqrt(R) / fr[:, None], "e4m3")
    return {
        "xt_words": xtp[0],
        "xt_scales": xtp[1],
        "w_words": wp[0],
        "w_scales": wp[1],
        "sa": (sgn((R, 1))).astype(np.float32),
        "sg": (0.25 * sgn((R, 1))).astype(np.float32),
        "lo": (np.random.uniform(-0.4, 0.4, (R, 1)) + np.log(fr)[:, None]).astype(np.float32),
        "wb_words": wbp[0],
        "wb_scales": wbp[1],
        "offs": striped(idx),
        "offs2": striped(idx2),
        "offs3": striped(idx3),
        "offs4": striped(idx4),
    }


def reference(xt_words, xt_scales, w_words, w_scales, sa, sg, lo, wb_words, wb_scales, offs, offs2, offs3, offs4):
    idx = unstriped(offs)
    idx2 = unstriped(offs2)
    idx3 = unstriped(offs3)
    idx4 = unstriped(offs4)
    xtu = unpack_weight(xt_words, xt_scales, "e4m3")
    wu = unpack_weight(w_words, w_scales, "e2m1")
    wbu = unpack_weight(wb_words, wb_scales, "e4m3")
    xtidxg = xtu[:, idx]
    a = wu.T @ xtidxg
    pw = np.zeros((R, C))
    pw[:, idx2] = a
    pg = np.maximum(pw, pw[:, idx3] * f64(sa))
    hid = np.exp(pg[:, idx4] * f64(sg) + f64(lo))
    hidq = mxq(hid, 0, "e4m3")
    p = wbu.T @ hidq
    return p

@@ -1,0 +1,177 @@
+from contextlib import ExitStack
+
+import concourse.mybir as mybir
+
+K, T, J, R, C, O, N = 512, 1024, 256, 512, 512, 256, 256
+FLOPS = 2 * K * R * J + 2 * R * N * O
+
+F32 = mybir.dt.float32
+BF16 = mybir.dt.bfloat16
+I32 = mybir.dt.int32
+U32 = mybir.dt.uint32
+U16 = mybir.dt.uint16
+U8 = mybir.dt.uint8
+FP8X4 = mybir.dt.float8_e4m3fn_x4
+FP4X4 = mybir.dt.float4_e2m1fn_x4
+COPY = mybir.ActivationFunctionType.Copy
+EXP = mybir.ActivationFunctionType.Exp
+MAX = mybir.AluOpType.max
+
+P = 128
+PACK = 4
+H = 128
+
+
+def tile_list_ladderexp_kernel(tc, xt_words, xt_scales, w_words, w_scales, sa, sg, lo, wb_words, wb_scales,
+                                  offs, offs2, offs3, offs4, out):
+    nc = tc.nc
+    with ExitStack() as ctx:
+        sb = ctx.enter_context(tc.tile_pool(name="sb", bufs=1))
+        ps = ctx.enter_context(tc.psum_pool(name="ps", bufs=1))
+
+        def tile(name, shape, dtype, tag=None):
+            return sb.tile(shape, dtype, name=name, tag=tag or name, align_bytes=64)
+
+        l1 = tile("l1", [P, J // 16], U16)
+        l2 = tile("l2", [P, J // 16], U16)
+        l3 = tile("l3", [P, C // 16], U16)
+        l4 = tile("l4", [P, O // 16], U16)
+        xw = tile("xw", [P, T], U32)
+        xs_stage = tile("xs_stage", [P, 2 * T], U8)
+        xs = tile("xs", [P, T], U8)
+        ww = tile("ww", [P, R], U16)
+        ws = tile("ws", [P, 2 * R], U8)
+        ww_d = tile("ww_d", [P, R], U16)
+        ws_d = tile("ws_d", [P, R], U8)
+        xg = tile("xg", [P, J], U32)
+        xgs = tile("xgs", [P, J], U8)
+        sa_t = tile("sa_t", [P, PACK], F32)
+        sg_t = tile("sg_t", [P, PACK], F32)
+        lo_t = tile("lo_t", [P, PACK], F32)
+        wbw = tile("wbw", [P, N], U32)
+        wbs = tile("wbs", [P, N], U8)
+        pw = [tile("pw%d" % t, [P, 2 * C], F32) for t in range(PACK)]
+        pg = {t: tile("pg%d" % t, [P, C], F32) for t in (0, 1, 3)}
+        prod = [tile("prod%d" % t, [P, C], F32) for t in range(PACK)]
+        a_sb = [tile("a%d" % t, [P, J], F32) for t in range(PACK - 1)]
+        hid = tile("hid", [P, PACK * O], BF16)
+        hc = tile("hc", [P, O], U32)
+        hs = tile("hs", [P, O], U8)
+
+        nc.vector.memset(ws[0:64, :].bitcast(I32), 0)
+        nc.vector.memset(xs_stage[0:64, :].bitcast(I32), 0)
+
+        nc.scalar.dma_start(xw[:].bitcast(I32), xt_words[0].rearrange("p t r -> p (t r)").bitcast(I32))
+        nc.sync.dma_start(ww[:].bitcast(I32), w_words[0].bitcast(I32))
+        xs_src = xt_scales[0].bitcast(I32).rearrange("(u q r) t -> q r u t", u=2, q=2)
+        ws_src = w_scales[0].bitcast(I32).rearrange("(u q r) t -> q r u t", u=2, q=2)
+        for q in range(2):
+            nc.sync.dma_start(ws[32 * q : 32 * q + 4, :].bitcast(I32).rearrange("p (u t) -> p u t", u=2), ws_src[q])
+        for q in range(2):
+            nc.sync.dma_start(xs_stage[32 * q : 32 * q + 4, :].bitcast(I32).rearrange("p (u t) -> p u t", u=2), xs_src[q])
+        nc.sync.dma_start(l1[:], offs)
+        nc.sync.dma_start(l2[:], offs2)
+        nc.sync.dma_start(l3[:], offs3)
+        nc.sync.dma_start(sa_t[:], sa.rearrange("(p t) o -> p (t o)", t=PACK))
+        nc.sync.dma_start(l4[:], offs4)
+        nc.sync.dma_start(sg_t[:], sg.rearrange("(p t) o -> p (t o)", t=PACK))
+        nc.sync.dma_start(lo_t[:], lo.rearrange("(p t) o -> p (t o)", t=PACK))
+        nc.sync.dma_start(wbw[:].bitcast(I32), wb_words[0].rearrange("p n r -> p (n r)").bitcast(I32))
+
+        for t in range(PACK):
+            nc.vector.memset(pw[t][:, 0:C], 0.0)
+        nc.vector.memset(wbs[:].bitcast(I32), 0)
+        for q in range(4):
+            nc.sync.dma_start(wbs[32 * q : 32 * q + 4, :].bitcast(I32), wb_scales[0, 4 * q : 4 * q + 4, :].bitcast(I32))
+
+        nc.scalar.copy(ww_d[:].rearrange("p (t m) -> p t m", t=PACK), ww[:].rearrange("p (m t) -> p t m", t=PACK))
+
+        nc.vector.tensor_copy(ws[64:128, 0:R].bitcast(I32), ws[0:64, R : 2 * R].bitcast(I32))
+        nc.vector.tensor_copy(xs[64:128, :].bitcast(I32), xs_stage[0:64, T : 2 * T].bitcast(I32))
+        nc.vector.tensor_copy(xs[0:64, :].bitcast(I32), xs_stage[0:64, 0:T].bitcast(I32))
+        nc.vector.tensor_copy(ws_d[:].rearrange("p (t m) -> p t m", t=PACK), ws[:, 0:R].rearrange("p (m t) -> p t m", t=PACK))
+        nc.vector.tensor_copy(xgs[:], xs[:].indirect(l1[:]))
+        for h in range(2):
+            nc.vector.tensor_copy(xg[:, h * H : (h + 1) * H], xw[:].indirect(l1[:, 8 * h : 8 * h + 8]))
+
+        def first_product(bank, t, cols):
+            m = slice(t * P, (t + 1) * P)
+            nc.tensor.matmul_mx(out=bank, lhsT=ww_d[:, m].bitcast(FP4X4), lhsT_scale=ws_d[:, m],
+                                rhs=xg[:, cols].bitcast(FP8X4), rhs_scale=xgs[:, cols], start=True, stop=True)
+
+        b0 = [ps.tile([P, 512], F32, name="b0%d" % h) for h in range(2)]
+        b = [None] + [ps.tile([P, 512], F32, name="b%d" % t) for t in range(1, PACK)]
+        for h in range(2):
+            first_product(b0[h][:, 0:H], 0, slice(h * H, (h + 1) * H))
+        for t in range(1, PACK):
+            first_product(b[t][:, 0:J], t, slice(0, J))
+
+        for h in range(2):
+            cols = slice(h * H, (h + 1) * H)
+            nc.vector.tensor_copy(a_sb[0][:, cols], b0[h][:, 0:H])
+            nc.scalar.activation(pw[0][:].indirect(l2[:, 8 * h : 8 * h + 8]), a_sb[0][:, cols], COPY)
+
+        def drain(t):
+            nc.vector.tensor_copy(a_sb[t][:], b[t][:, 0:J])
+
+        def put(t):
+            nc.vector.tensor_copy(pw[t][:].indirect(l2[:]), a_sb[t][:])
+
+        def fetch(t, c0, c1):
+            nc.scalar.activation(prod[t][:, c0:c1], pw[t][:].indirect(l3[:, c0 // 16 : c1 // 16]), COPY, scale=sa_t[:, t : t + 1])
+
+        def keep(t, c0, c1):
+            nc.vector.tensor_tensor(pg[t][:, c0:c1], pw[t][:, c0:c1], prod[t][:, c0:c1], MAX)
+
+        def look(t, o0, o1):
+            nc.scalar.activation(hid[:, PACK * o0 + t : PACK * o1 : PACK], pg[t][:].indirect(l4[:, o0 // 16 : o1 // 16]),
+                                 EXP, bias=lo_t[:, t : t + 1], scale=sg_t[:, t : t + 1])
+
+        drain(1)
+        drain(2)
+        put(1)
+        put(2)
+        fetch(0, 0, C)
+        fetch(1, 0, C)
+        fetch(2, 0, C)
+        keep(0, 0, C)
+        a_sb.append(tile("a3", [P, J], F32, tag="prod0"))
+        nc.scalar.copy(a_sb[3][:], b[3][:, 0:J])
+        keep(1, 0, C)
+        put(3)
+        look(0, 0, O)
+        look(1, 0, O)
+        pg[2] = tile("pg2", [P, C], F32, tag="prod0")
+        keep(2, 0, C)
+        fetch(3, 0, C // 2)
+        fetch(3, C // 2, C)
+        keep(3, 0, C // 2)
+        keep(3, C // 2, C)
+        look(2, 0, O)
+        look(3, 0, H)
+        look(3, H, O)
+
+        out_v = out.rearrange("(h p) o -> p h o", p=P)
+        for g in range(2):
+            cols = slice(g * H, (g + 1) * H)
+            nc.vector.quantize_mx(out=hc[:, cols].bitcast(FP8X4), scales=hs[:, cols], in_=hid[:, PACK * g * H : PACK * (g + 1) * H])
+        oa = ps.tile([P, 512], F32, name="oa")
+        ob = [ps.tile([P, 512], F32, name="ob%d" % h) for h in range(2)]
+
+        def second_product(bank, h, cols):
+            n = slice(h * P, (h + 1) * P)
+            nc.tensor.matmul_mx(out=bank, lhsT=wbw[:, n].bitcast(FP8X4), lhsT_scale=wbs[:, n],
+                                rhs=hc[:, cols].bitcast(FP8X4), rhs_scale=hs[:, cols], start=True, stop=True)
+
+        for h in range(2):
+            second_product(oa[:, h * H : (h + 1) * H], h, slice(0, H))
+        for h in range(2):
+            second_product(ob[h][:, 0:H], h, slice(H, O))
+        ra = tile("ra", [P, 2 * H], F32)
+        nc.vector.tensor_copy(ra[:], oa[:, 0 : 2 * H])
+        nc.sync.dma_start(out_v[:, :, 0:H], ra[:].rearrange("p (h o) -> p h o", h=2))
+        rb = [tile("rb%d" % h, [P, H], F32) for h in range(2)]
+        nc.vector.tensor_copy(rb[0][:], ob[0][:, 0:H])
+        nc.sync.dma_start(out[0:P, H:O], rb[0][:])
+        nc.scalar.copy(rb[1][:], ob[1][:, 0:H])
+        nc.scalar.dma_start(out[P : 2 * P, H:O], rb[1][:])

@@ -58,18 +58,18 @@ def tile_list_ladderexp_kernel(tc, xt_words, xt_scales, w_words, w_scales, sa, s
         hc = tile("hc", [P, O], U32)
         hs = tile("hs", [P, O], U8)
 
-        nc.vector.memset(ws[0:64, :].bitcast(I32), 0)
+        nc.vector.memset(ws[64:128, :].bitcast(I32), 0)
         nc.vector.memset(xs_stage[0:64, :].bitcast(I32), 0)
 
-        nc.scalar.dma_start(xw[:].bitcast(I32), xt_words[0].rearrange("p t r -> p (t r)").bitcast(I32))
         nc.sync.dma_start(ww[:].bitcast(I32), w_words[0].bitcast(I32))
         xs_src = xt_scales[0].bitcast(I32).rearrange("(u q r) t -> q r u t", u=2, q=2)
         ws_src = w_scales[0].bitcast(I32).rearrange("(u q r) t -> q r u t", u=2, q=2)
         for q in range(2):
-            nc.sync.dma_start(ws[32 * q : 32 * q + 4, :].bitcast(I32).rearrange("p (u t) -> p u t", u=2), ws_src[q])
+            nc.sync.dma_start(ws[64 + 32 * q : 64 + 32 * q + 4, :].bitcast(I32).rearrange("p (u t) -> p u t", u=2), ws_src[q])
         for q in range(2):
             nc.sync.dma_start(xs_stage[32 * q : 32 * q + 4, :].bitcast(I32).rearrange("p (u t) -> p u t", u=2), xs_src[q])
         nc.sync.dma_start(l1[:], offs)
+        nc.sync.dma_start(xw[:].bitcast(I32), xt_words[0].rearrange("p t r -> p (t r)").bitcast(I32))
         nc.sync.dma_start(l2[:], offs2)
         nc.sync.dma_start(l3[:], offs3)
         nc.sync.dma_start(sa_t[:], sa.rearrange("(p t) o -> p (t o)", t=PACK))
@@ -86,10 +86,10 @@ def tile_list_ladderexp_kernel(tc, xt_words, xt_scales, w_words, w_scales, sa, s
 
         nc.scalar.copy(ww_d[:].rearrange("p (t m) -> p t m", t=PACK), ww[:].rearrange("p (m t) -> p t m", t=PACK))
 
-        nc.vector.tensor_copy(ws[64:128, 0:R].bitcast(I32), ws[0:64, R : 2 * R].bitcast(I32))
-        nc.vector.tensor_copy(xs[64:128, :].bitcast(I32), xs_stage[0:64, T : 2 * T].bitcast(I32))
+        nc.vector.tensor_copy(ws[0:64, R : 2 * R].bitcast(I32), ws[64:128, 0:R].bitcast(I32))
         nc.vector.tensor_copy(xs[0:64, :].bitcast(I32), xs_stage[0:64, 0:T].bitcast(I32))
-        nc.vector.tensor_copy(ws_d[:].rearrange("p (t m) -> p t m", t=PACK), ws[:, 0:R].rearrange("p (m t) -> p t m", t=PACK))
+        nc.vector.tensor_copy(xs[64:128, :].bitcast(I32), xs_stage[0:64, T : 2 * T].bitcast(I32))
+        nc.vector.tensor_copy(ws_d[:].rearrange("p (t m) -> p t m", t=PACK), ws[:, R : 2 * R].rearrange("p (m t) -> p t m", t=PACK))
         nc.vector.tensor_copy(xgs[:], xs[:].indirect(l1[:]))
         for h in range(2):
             nc.vector.tensor_copy(xg[:, h * H : (h + 1) * H], xw[:].indirect(l1[:, 8 * h : 8 * h + 8]))

@@ -37,10 +37,10 @@ def tile_list_ladderexp_kernel(tc, xt_words, xt_scales, w_words, w_scales, sa, s
         l3 = tile("l3", [P, C // 16], U16)
         l4 = tile("l4", [P, O // 16], U16)
         xw = tile("xw", [P, T], U32)
-        xs_stage = tile("xs_stage", [P, 2 * T], U8)
+        ws_stage = tile("ws_stage", [4, 4 * R], U8)
         xs = tile("xs", [P, T], U8)
         ww = tile("ww", [P, R], U16)
-        ws = tile("ws", [P, 2 * R], U8)
+        ws = tile("ws", [P, R], U8)
         ww_d = tile("ww_d", [P, R], U16)
         ws_d = tile("ws_d", [P, R], U8)
         xg = tile("xg", [P, J], U32)
@@ -50,25 +50,24 @@ def tile_list_ladderexp_kernel(tc, xt_words, xt_scales, w_words, w_scales, sa, s
         lo_t = tile("lo_t", [P, PACK], F32)
         wbw = tile("wbw", [P, N], U32)
         wbs = tile("wbs", [P, N], U8)
-        pw = [tile("pw%d" % t, [P, 2 * C], F32) for t in range(PACK)]
-        pg = {t: tile("pg%d" % t, [P, C], F32) for t in (0, 1, 3)}
+        pw = [tile("pw%d" % t, [P, 2 * C], F32) for t in range(PACK - 1)]
+        pw.append(pw[0])
+        pg = [tile("pg%d" % t, [P, C], F32) for t in range(PACK)]
         prod = [tile("prod%d" % t, [P, C], F32) for t in range(PACK)]
-        a_sb = [tile("a%d" % t, [P, J], F32) for t in range(PACK - 1)]
+        a_sb = [tile("a%d" % t, [P, J], F32) for t in range(PACK)]
         hid = tile("hid", [P, PACK * O], BF16)
         hc = tile("hc", [P, O], U32)
         hs = tile("hs", [P, O], U8)
 
-        nc.vector.memset(ws[64:128, :].bitcast(I32), 0)
-        nc.vector.memset(xs_stage[0:64, :].bitcast(I32), 0)
+        nc.vector.memset(xs[:].bitcast(I32), 0)
+        nc.vector.memset(ws[:].bitcast(I32), 0)
 
-        nc.sync.dma_start(ww[:].bitcast(I32), w_words[0].bitcast(I32))
-        xs_src = xt_scales[0].bitcast(I32).rearrange("(u q r) t -> q r u t", u=2, q=2)
-        ws_src = w_scales[0].bitcast(I32).rearrange("(u q r) t -> q r u t", u=2, q=2)
-        for q in range(2):
-            nc.sync.dma_start(ws[64 + 32 * q : 64 + 32 * q + 4, :].bitcast(I32).rearrange("p (u t) -> p u t", u=2), ws_src[q])
-        for q in range(2):
-            nc.sync.dma_start(xs_stage[32 * q : 32 * q + 4, :].bitcast(I32).rearrange("p (u t) -> p u t", u=2), xs_src[q])
+        nc.sync.dma_start(ws_stage[:].bitcast(I32).rearrange("r (q c) -> r q c", q=4),
+                          w_scales[0].bitcast(I32).rearrange("(q r) c -> r q c", r=4))
         nc.sync.dma_start(l1[:], offs)
+        nc.sync.dma_start(ww[:].bitcast(I32), w_words[0].bitcast(I32))
+        for r in range(4):
+            nc.sync.dma_start(xs[r:P:32, :].bitcast(I32), xt_scales[0, r:16:4, :].bitcast(I32))
         nc.sync.dma_start(xw[:].bitcast(I32), xt_words[0].rearrange("p t r -> p (t r)").bitcast(I32))
         nc.sync.dma_start(l2[:], offs2)
         nc.sync.dma_start(l3[:], offs3)
@@ -78,19 +77,18 @@ def tile_list_ladderexp_kernel(tc, xt_words, xt_scales, w_words, w_scales, sa, s
         nc.sync.dma_start(lo_t[:], lo.rearrange("(p t) o -> p (t o)", t=PACK))
         nc.sync.dma_start(wbw[:].bitcast(I32), wb_words[0].rearrange("p n r -> p (n r)").bitcast(I32))
 
-        for t in range(PACK):
+        for t in range(PACK - 1):
             nc.vector.memset(pw[t][:, 0:C], 0.0)
         nc.vector.memset(wbs[:].bitcast(I32), 0)
-        for q in range(4):
-            nc.sync.dma_start(wbs[32 * q : 32 * q + 4, :].bitcast(I32), wb_scales[0, 4 * q : 4 * q + 4, :].bitcast(I32))
+        for r in range(4):
+            nc.sync.dma_start(wbs[r:P:32, :].bitcast(I32), wb_scales[0, r:16:4, :].bitcast(I32))
 
         nc.scalar.copy(ww_d[:].rearrange("p (t m) -> p t m", t=PACK), ww[:].rearrange("p (m t) -> p t m", t=PACK))
 
-        nc.vector.tensor_copy(ws[0:64, R : 2 * R].bitcast(I32), ws[64:128, 0:R].bitcast(I32))
-        nc.vector.tensor_copy(xs[0:64, :].bitcast(I32), xs_stage[0:64, 0:T].bitcast(I32))
-        nc.vector.tensor_copy(xs[64:128, :].bitcast(I32), xs_stage[0:64, T : 2 * T].bitcast(I32))
-        nc.vector.tensor_copy(ws_d[:].rearrange("p (t m) -> p t m", t=PACK), ws[:, R : 2 * R].rearrange("p (m t) -> p t m", t=PACK))
+        for q in range(4):
+            nc.vector.tensor_copy(ws[32 * q : 32 * q + 4, :].bitcast(I32), ws_stage[:, q * R : (q + 1) * R].bitcast(I32))
         nc.vector.tensor_copy(xgs[:], xs[:].indirect(l1[:]))
+        nc.vector.tensor_copy(ws_d[:].rearrange("p (t m) -> p t m", t=PACK), ws[:].rearrange("p (m t) -> p t m", t=PACK))
         for h in range(2):
             nc.vector.tensor_copy(xg[:, h * H : (h + 1) * H], xw[:].indirect(l1[:, 8 * h : 8 * h + 8]))
 
@@ -100,19 +98,21 @@ def tile_list_ladderexp_kernel(tc, xt_words, xt_scales, w_words, w_scales, sa, s
                                 rhs=xg[:, cols].bitcast(FP8X4), rhs_scale=xgs[:, cols], start=True, stop=True)
 
         b0 = [ps.tile([P, 512], F32, name="b0%d" % h) for h in range(2)]
-        b = [None] + [ps.tile([P, 512], F32, name="b%d" % t) for t in range(1, PACK)]
-        for h in range(2):
-            first_product(b0[h][:, 0:H], 0, slice(h * H, (h + 1) * H))
-        for t in range(1, PACK):
-            first_product(b[t][:, 0:J], t, slice(0, J))
+        b1 = ps.tile([P, 512], F32, name="b1")
+        b2 = ps.tile([P, 512], F32, name="b2")
+        first_product(b0[0][:, 0:H], 0, slice(0, H))
+        first_product(b1[:, 0:J], 1, slice(0, J))
+        first_product(b2[:, 0:J], 2, slice(0, J))
+        first_product(b0[1][:, 0:H], 0, slice(H, J))
 
-        for h in range(2):
-            cols = slice(h * H, (h + 1) * H)
-            nc.vector.tensor_copy(a_sb[0][:, cols], b0[h][:, 0:H])
-            nc.scalar.activation(pw[0][:].indirect(l2[:, 8 * h : 8 * h + 8]), a_sb[0][:, cols], COPY)
-
-        def drain(t):
-            nc.vector.tensor_copy(a_sb[t][:], b[t][:, 0:J])
+        nc.vector.tensor_copy(a_sb[0][:, 0:H], b0[0][:, 0:H])
+        nc.scalar.activation(pw[0][:].indirect(l2[:, 0:8]), a_sb[0][:, 0:H], COPY)
+        nc.vector.tensor_copy(a_sb[1][:], b1[:, 0:J])
+        nc.scalar.copy(a_sb[2][:], b2[:, 0:J])
+        nc.vector.tensor_copy(a_sb[0][:, H:J], b0[1][:, 0:H])
+        nc.scalar.activation(pw[0][:].indirect(l2[:, 8:16]), a_sb[0][:, H:J], COPY)
+        first_product(b0[1][:, 0:J], 3, slice(0, J))
+        nc.scalar.copy(a_sb[3][:], b0[1][:, 0:J])
 
         def put(t):
             nc.vector.tensor_copy(pw[t][:].indirect(l2[:]), a_sb[t][:])
@@ -127,21 +127,16 @@ def tile_list_ladderexp_kernel(tc, xt_words, xt_scales, w_words, w_scales, sa, s
             nc.scalar.activation(hid[:, PACK * o0 + t : PACK * o1 : PACK], pg[t][:].indirect(l4[:, o0 // 16 : o1 // 16]),
                                  EXP, bias=lo_t[:, t : t + 1], scale=sg_t[:, t : t + 1])
 
-        drain(1)
-        drain(2)
         put(1)
         put(2)
         fetch(0, 0, C)
         fetch(1, 0, C)
         fetch(2, 0, C)
         keep(0, 0, C)
-        a_sb.append(tile("a3", [P, J], F32, tag="prod0"))
-        nc.scalar.copy(a_sb[3][:], b[3][:, 0:J])
         keep(1, 0, C)
         put(3)
         look(0, 0, O)
         look(1, 0, O)
-        pg[2] = tile("pg2", [P, C], F32, tag="prod0")
         keep(2, 0, C)
         fetch(3, 0, C // 2)
         fetch(3, C // 2, C)

@@ -19,154 +19,179 @@ MAX = mybir.AluOpType.max
 
 P = 128
 PACK = 4
-H = 128
+QUADRANT = 32
+SCALE_ROWS = 4
+PER_COLUMN = 16
+BANK = 512
+HALF = 128
+LAST = PACK - 1
 
 
 def tile_list_ladderexp_kernel(tc, xt_words, xt_scales, w_words, w_scales, sa, sg, lo, wb_words, wb_scales,
                                   offs, offs2, offs3, offs4, out):
     nc = tc.nc
     with ExitStack() as ctx:
-        sb = ctx.enter_context(tc.tile_pool(name="sb", bufs=1))
-        ps = ctx.enter_context(tc.psum_pool(name="ps", bufs=1))
+        sbuf = ctx.enter_context(tc.tile_pool(name="sbuf", bufs=1))
+        psum = ctx.enter_context(tc.psum_pool(name="psum", bufs=1))
 
-        def tile(name, shape, dtype, tag=None):
-            return sb.tile(shape, dtype, name=name, tag=tag or name, align_bytes=64)
+        def tile(name, shape, dtype):
+            return sbuf.tile(shape, dtype, name=name, align_bytes=64)
 
-        l1 = tile("l1", [P, J // 16], U16)
-        l2 = tile("l2", [P, J // 16], U16)
-        l3 = tile("l3", [P, C // 16], U16)
-        l4 = tile("l4", [P, O // 16], U16)
-        xw = tile("xw", [P, T], U32)
-        ws_stage = tile("ws_stage", [4, 4 * R], U8)
-        xs = tile("xs", [P, T], U8)
-        ww = tile("ww", [P, R], U16)
-        ws = tile("ws", [P, R], U8)
-        ww_d = tile("ww_d", [P, R], U16)
-        ws_d = tile("ws_d", [P, R], U8)
-        xg = tile("xg", [P, J], U32)
-        xgs = tile("xgs", [P, J], U8)
-        sa_t = tile("sa_t", [P, PACK], F32)
-        sg_t = tile("sg_t", [P, PACK], F32)
-        lo_t = tile("lo_t", [P, PACK], F32)
-        wbw = tile("wbw", [P, N], U32)
-        wbs = tile("wbs", [P, N], U8)
-        pw = [tile("pw%d" % t, [P, 2 * C], F32) for t in range(PACK - 1)]
-        pw.append(pw[0])
-        pg = [tile("pg%d" % t, [P, C], F32) for t in range(PACK)]
-        prod = [tile("prod%d" % t, [P, C], F32) for t in range(PACK)]
-        a_sb = [tile("a%d" % t, [P, J], F32) for t in range(PACK)]
+        def bank(name):
+            return psum.tile([P, BANK], F32, name=name)
+
+        def entries(list_tile, first, end):
+            return list_tile[:, first // PER_COLUMN : end // PER_COLUMN]
+
+        token_list = tile("token_list", [P, J // PER_COLUMN], U16)
+        put_list = tile("put_list", [P, J // PER_COLUMN], U16)
+        fetch_list = tile("fetch_list", [P, C // PER_COLUMN], U16)
+        place_list = tile("place_list", [P, O // PER_COLUMN], U16)
+        x_words = tile("x_words", [P, T], U32)
+        w_scale_rows = tile("w_scale_rows", [SCALE_ROWS, SCALE_ROWS * R], U8)
+        x_plane = tile("x_plane", [P, T], U8)
+        w_packed = tile("w_packed", [P, R], U16)
+        w_plane = tile("w_plane", [P, R], U8)
+        w_dealt = tile("w_dealt", [P, R], U16)
+        w_plane_dealt = tile("w_plane_dealt", [P, R], U8)
+        picked_words = tile("picked_words", [P, J], U32)
+        picked_plane = tile("picked_plane", [P, J], U8)
+        weight = tile("weight", [P, PACK], F32)
+        slope = tile("slope", [P, PACK], F32)
+        level = tile("level", [P, PACK], F32)
+        wb_packed = tile("wb_packed", [P, N], U32)
+        wb_plane = tile("wb_plane", [P, N], U8)
+        board = [tile("board%d" % s, [P, 2 * C], F32) for s in range(LAST)]
+        board.append(board[0])
+        kept = [tile("kept%d" % s, [P, C], F32) for s in range(PACK)]
+        fetched = [tile("fetched%d" % s, [P, C], F32) for s in range(PACK)]
+        hidden = [tile("hidden%d" % s, [P, J], F32) for s in range(LAST)]
+        hidden.append(kept[LAST - 1][:, 0:J])
         hid = tile("hid", [P, PACK * O], BF16)
-        hc = tile("hc", [P, O], U32)
-        hs = tile("hs", [P, O], U8)
+        hid_words = tile("hid_words", [P, O], U32)
+        hid_plane = tile("hid_plane", [P, O], U8)
 
-        nc.vector.memset(xs[:].bitcast(I32), 0)
-        nc.vector.memset(ws[:].bitcast(I32), 0)
+        def load_plane(plane, scales):
+            for i in range(SCALE_ROWS):
+                nc.sync.dma_start(plane[i:P:QUADRANT, :].bitcast(I32), scales[0, i : SCALE_ROWS * SCALE_ROWS : SCALE_ROWS, :].bitcast(I32))
 
-        nc.sync.dma_start(ws_stage[:].bitcast(I32).rearrange("r (q c) -> r q c", q=4),
-                          w_scales[0].bitcast(I32).rearrange("(q r) c -> r q c", r=4))
-        nc.sync.dma_start(l1[:], offs)
-        nc.sync.dma_start(ww[:].bitcast(I32), w_words[0].bitcast(I32))
-        for r in range(4):
-            nc.sync.dma_start(xs[r:P:32, :].bitcast(I32), xt_scales[0, r:16:4, :].bitcast(I32))
-        nc.sync.dma_start(xw[:].bitcast(I32), xt_words[0].rearrange("p t r -> p (t r)").bitcast(I32))
-        nc.sync.dma_start(l2[:], offs2)
-        nc.sync.dma_start(l3[:], offs3)
-        nc.sync.dma_start(sa_t[:], sa.rearrange("(p t) o -> p (t o)", t=PACK))
-        nc.sync.dma_start(l4[:], offs4)
-        nc.sync.dma_start(sg_t[:], sg.rearrange("(p t) o -> p (t o)", t=PACK))
-        nc.sync.dma_start(lo_t[:], lo.rearrange("(p t) o -> p (t o)", t=PACK))
-        nc.sync.dma_start(wbw[:].bitcast(I32), wb_words[0].rearrange("p n r -> p (n r)").bitcast(I32))
+        nc.vector.memset(x_plane[:].bitcast(I32), 0)
+        nc.vector.memset(w_plane[:].bitcast(I32), 0)
 
-        for t in range(PACK - 1):
-            nc.vector.memset(pw[t][:, 0:C], 0.0)
-        nc.vector.memset(wbs[:].bitcast(I32), 0)
-        for r in range(4):
-            nc.sync.dma_start(wbs[r:P:32, :].bitcast(I32), wb_scales[0, r:16:4, :].bitcast(I32))
+        nc.sync.dma_start(w_scale_rows[:].bitcast(I32).rearrange("i (q c) -> i q c", q=SCALE_ROWS),
+                          w_scales[0].bitcast(I32).rearrange("(q i) c -> i q c", i=SCALE_ROWS))
+        nc.sync.dma_start(token_list[:], offs)
+        nc.sync.dma_start(w_packed[:].bitcast(I32), w_words[0].bitcast(I32))
+        load_plane(x_plane, xt_scales)
+        nc.sync.dma_start(x_words[:].bitcast(I32), xt_words[0].rearrange("p t i -> p (t i)").bitcast(I32))
+        nc.sync.dma_start(put_list[:], offs2)
+        nc.sync.dma_start(fetch_list[:], offs3)
+        nc.sync.dma_start(weight[:], sa.rearrange("(p s) o -> p (s o)", s=PACK))
+        nc.sync.dma_start(place_list[:], offs4)
+        nc.sync.dma_start(slope[:], sg.rearrange("(p s) o -> p (s o)", s=PACK))
+        nc.sync.dma_start(level[:], lo.rearrange("(p s) o -> p (s o)", s=PACK))
+        nc.sync.dma_start(wb_packed[:].bitcast(I32), wb_words[0].rearrange("p n i -> p (n i)").bitcast(I32))
 
-        nc.scalar.copy(ww_d[:].rearrange("p (t m) -> p t m", t=PACK), ww[:].rearrange("p (m t) -> p t m", t=PACK))
+        for s in range(LAST):
+            nc.vector.memset(board[s][:, 0:C], 0.0)
+        nc.vector.memset(wb_plane[:].bitcast(I32), 0)
+        load_plane(wb_plane, wb_scales)
 
-        for q in range(4):
-            nc.vector.tensor_copy(ws[32 * q : 32 * q + 4, :].bitcast(I32), ws_stage[:, q * R : (q + 1) * R].bitcast(I32))
-        nc.vector.tensor_copy(xgs[:], xs[:].indirect(l1[:]))
-        nc.vector.tensor_copy(ws_d[:].rearrange("p (t m) -> p t m", t=PACK), ws[:].rearrange("p (m t) -> p t m", t=PACK))
+        nc.scalar.copy(w_dealt[:].rearrange("p (s m) -> p s m", s=PACK), w_packed[:].rearrange("p (m s) -> p s m", s=PACK))
+
+        for q in range(SCALE_ROWS):
+            nc.vector.tensor_copy(w_plane[QUADRANT * q : QUADRANT * q + SCALE_ROWS, :].bitcast(I32),
+                                  w_scale_rows[:, q * R : (q + 1) * R].bitcast(I32))
+        plane_by_slice = w_plane[:].rearrange("p (m s) -> p s m", s=PACK)
+        dealt_by_slice = w_plane_dealt[:].rearrange("p (s m) -> p s m", s=PACK)
+        nc.vector.tensor_copy(picked_plane[:, 0:HALF], x_plane[:].indirect(entries(token_list, 0, HALF)))
+        nc.vector.tensor_copy(dealt_by_slice[:, 0, :], plane_by_slice[:, 0, :])
+        nc.vector.tensor_copy(picked_words[:, 0:HALF], x_words[:].indirect(entries(token_list, 0, HALF)))
+        nc.vector.tensor_copy(picked_plane[:, HALF:J], x_plane[:].indirect(entries(token_list, HALF, J)))
+        nc.vector.tensor_copy(picked_words[:, HALF:J], x_words[:].indirect(entries(token_list, HALF, J)))
+        nc.vector.tensor_copy(dealt_by_slice[:, 1:PACK, :], plane_by_slice[:, 1:PACK, :])
+
+        def first_product(acc, s, first, end):
+            features = slice(s * P, (s + 1) * P)
+            nc.tensor.matmul_mx(out=acc[:, 0 : end - first], lhsT=w_dealt[:, features].bitcast(FP4X4),
+                                lhsT_scale=w_plane_dealt[:, features], rhs=picked_words[:, first:end].bitcast(FP8X4),
+                                rhs_scale=picked_plane[:, first:end], start=True, stop=True)
+
+        half_acc = [bank("half_acc%d" % h) for h in range(2)]
+        slice_acc = {s: bank("slice_acc%d" % s) for s in range(1, PACK)}
         for h in range(2):
-            nc.vector.tensor_copy(xg[:, h * H : (h + 1) * H], xw[:].indirect(l1[:, 8 * h : 8 * h + 8]))
+            first_product(half_acc[h], 0, h * HALF, (h + 1) * HALF)
+        for s in range(1, PACK):
+            first_product(slice_acc[s], s, 0, J)
 
-        def first_product(bank, t, cols):
-            m = slice(t * P, (t + 1) * P)
-            nc.tensor.matmul_mx(out=bank, lhsT=ww_d[:, m].bitcast(FP4X4), lhsT_scale=ws_d[:, m],
-                                rhs=xg[:, cols].bitcast(FP8X4), rhs_scale=xgs[:, cols], start=True, stop=True)
+        nc.scalar.copy(hidden[0][:, 0:HALF], half_acc[0][:, 0:HALF])
+        nc.scalar.activation(board[0][:].indirect(entries(put_list, 0, HALF)), hidden[0][:, 0:HALF], COPY)
+        nc.vector.tensor_copy(hidden[0][:, HALF:J], half_acc[1][:, 0:HALF])
+        nc.scalar.activation(board[0][:].indirect(entries(put_list, HALF, J)), hidden[0][:, HALF:J], COPY)
 
-        b0 = [ps.tile([P, 512], F32, name="b0%d" % h) for h in range(2)]
-        b1 = ps.tile([P, 512], F32, name="b1")
-        b2 = ps.tile([P, 512], F32, name="b2")
-        first_product(b0[0][:, 0:H], 0, slice(0, H))
-        first_product(b1[:, 0:J], 1, slice(0, J))
-        first_product(b2[:, 0:J], 2, slice(0, J))
-        first_product(b0[1][:, 0:H], 0, slice(H, J))
+        def drain(s):
+            nc.vector.tensor_copy(hidden[s][:, 0:J], slice_acc[s][:, 0:J])
 
-        nc.vector.tensor_copy(a_sb[0][:, 0:H], b0[0][:, 0:H])
-        nc.scalar.activation(pw[0][:].indirect(l2[:, 0:8]), a_sb[0][:, 0:H], COPY)
-        nc.vector.tensor_copy(a_sb[1][:], b1[:, 0:J])
-        nc.scalar.copy(a_sb[2][:], b2[:, 0:J])
-        nc.vector.tensor_copy(a_sb[0][:, H:J], b0[1][:, 0:H])
-        nc.scalar.activation(pw[0][:].indirect(l2[:, 8:16]), a_sb[0][:, H:J], COPY)
-        first_product(b0[1][:, 0:J], 3, slice(0, J))
-        nc.scalar.copy(a_sb[3][:], b0[1][:, 0:J])
+        def put(s):
+            nc.vector.tensor_copy(board[s][:].indirect(put_list[:]), hidden[s][:, 0:J])
 
-        def put(t):
-            nc.vector.tensor_copy(pw[t][:].indirect(l2[:]), a_sb[t][:])
+        def fetch(s, first, end):
+            nc.scalar.activation(fetched[s][:, first:end], board[s][:].indirect(entries(fetch_list, first, end)),
+                                 COPY, scale=weight[:, s : s + 1])
 
-        def fetch(t, c0, c1):
-            nc.scalar.activation(prod[t][:, c0:c1], pw[t][:].indirect(l3[:, c0 // 16 : c1 // 16]), COPY, scale=sa_t[:, t : t + 1])
+        def keep(s, first, end):
+            nc.vector.tensor_tensor(kept[s][:, first:end], board[s][:, first:end], fetched[s][:, first:end], MAX)
 
-        def keep(t, c0, c1):
-            nc.vector.tensor_tensor(pg[t][:, c0:c1], pw[t][:, c0:c1], prod[t][:, c0:c1], MAX)
+        def look(s, first, end):
+            nc.scalar.activation(hid[:, PACK * first + s : PACK * end : PACK],
+                                 kept[s][:].indirect(entries(place_list, first, end)),
+                                 EXP, bias=level[:, s : s + 1], scale=slope[:, s : s + 1])
 
-        def look(t, o0, o1):
-            nc.scalar.activation(hid[:, PACK * o0 + t : PACK * o1 : PACK], pg[t][:].indirect(l4[:, o0 // 16 : o1 // 16]),
-                                 EXP, bias=lo_t[:, t : t + 1], scale=sg_t[:, t : t + 1])
+        middle = range(1, LAST)
+        for s in middle:
+            drain(s)
+        for s in middle:
+            put(s)
+        drain(LAST)
+        for s in range(LAST):
+            fetch(s, 0, C)
+        for s in range(LAST - 1):
+            keep(s, 0, C)
+        put(LAST)
+        for s in range(LAST - 1):
+            look(s, 0, O)
+        keep(LAST - 1, 0, C)
 
-        put(1)
-        put(2)
-        fetch(0, 0, C)
-        fetch(1, 0, C)
-        fetch(2, 0, C)
-        keep(0, 0, C)
-        keep(1, 0, C)
-        put(3)
-        look(0, 0, O)
-        look(1, 0, O)
-        keep(2, 0, C)
-        fetch(3, 0, C // 2)
-        fetch(3, C // 2, C)
-        keep(3, 0, C // 2)
-        keep(3, C // 2, C)
-        look(2, 0, O)
-        look(3, 0, H)
-        look(3, H, O)
+        for first in (0, C // 2):
+            fetch(LAST, first, first + C // 2)
+        for first in (0, C // 2):
+            keep(LAST, first, first + C // 2)
+        look(LAST - 1, 0, O)
+        for first in (0, HALF):
+            look(LAST, first, first + HALF)
 
-        out_v = out.rearrange("(h p) o -> p h o", p=P)
-        for g in range(2):
-            cols = slice(g * H, (g + 1) * H)
-            nc.vector.quantize_mx(out=hc[:, cols].bitcast(FP8X4), scales=hs[:, cols], in_=hid[:, PACK * g * H : PACK * (g + 1) * H])
-        oa = ps.tile([P, 512], F32, name="oa")
-        ob = [ps.tile([P, 512], F32, name="ob%d" % h) for h in range(2)]
+        for first in (0, HALF):
+            places = slice(first, first + HALF)
+            nc.vector.quantize_mx(out=hid_words[:, places].bitcast(FP8X4), scales=hid_plane[:, places],
+                                  in_=hid[:, PACK * first : PACK * (first + HALF)])
 
-        def second_product(bank, h, cols):
-            n = slice(h * P, (h + 1) * P)
-            nc.tensor.matmul_mx(out=bank, lhsT=wbw[:, n].bitcast(FP8X4), lhsT_scale=wbs[:, n],
-                                rhs=hc[:, cols].bitcast(FP8X4), rhs_scale=hs[:, cols], start=True, stop=True)
+        def second_product(acc, h, places):
+            rows = slice(h * P, (h + 1) * P)
+            nc.tensor.matmul_mx(out=acc, lhsT=wb_packed[:, rows].bitcast(FP8X4), lhsT_scale=wb_plane[:, rows],
+                                rhs=hid_words[:, places].bitcast(FP8X4), rhs_scale=hid_plane[:, places],
+                                start=True, stop=True)
 
+        early_acc = bank("early_acc")
+        late_acc = [bank("late_acc%d" % h) for h in range(2)]
         for h in range(2):
-            second_product(oa[:, h * H : (h + 1) * H], h, slice(0, H))
+            second_product(early_acc[:, h * HALF : (h + 1) * HALF], h, slice(0, HALF))
         for h in range(2):
-            second_product(ob[h][:, 0:H], h, slice(H, O))
-        ra = tile("ra", [P, 2 * H], F32)
-        nc.vector.tensor_copy(ra[:], oa[:, 0 : 2 * H])
-        nc.sync.dma_start(out_v[:, :, 0:H], ra[:].rearrange("p (h o) -> p h o", h=2))
-        rb = [tile("rb%d" % h, [P, H], F32) for h in range(2)]
-        nc.vector.tensor_copy(rb[0][:], ob[0][:, 0:H])
-        nc.sync.dma_start(out[0:P, H:O], rb[0][:])
-        nc.scalar.copy(rb[1][:], ob[1][:, 0:H])
-        nc.scalar.dma_start(out[P : 2 * P, H:O], rb[1][:])
+            second_product(late_acc[h][:, 0:HALF], h, slice(HALF, O))
+        early = tile("early", [P, 2 * HALF], F32)
+        nc.vector.tensor_copy(early[:], early_acc[:, 0 : 2 * HALF])
+        nc.sync.dma_start(out.rearrange("(h p) o -> p h o", p=P)[:, :, 0:HALF], early[:].rearrange("p (h o) -> p h o", h=2))
+        late = [tile("late%d" % h, [P, HALF], F32) for h in range(2)]
+        nc.vector.tensor_copy(late[0][:], late_acc[0][:, 0:HALF])
+        nc.sync.dma_start(out[0:P, HALF:O], late[0][:])
+        nc.scalar.copy(late[1][:], late_acc[1][:, 0:HALF])
+        nc.scalar.dma_start(out[P : 2 * P, HALF:O], late[1][:])

from contextlib import ExitStack

import concourse.mybir as mybir

K, T, J, R, C, O, N = 512, 1024, 256, 512, 512, 256, 256
FLOPS = 2 * K * R * J + 2 * R * N * O

F32 = mybir.dt.float32
BF16 = mybir.dt.bfloat16
I32 = mybir.dt.int32
U32 = mybir.dt.uint32
U16 = mybir.dt.uint16
U8 = mybir.dt.uint8
FP8X4 = mybir.dt.float8_e4m3fn_x4
FP4X4 = mybir.dt.float4_e2m1fn_x4
COPY = mybir.ActivationFunctionType.Copy
EXP = mybir.ActivationFunctionType.Exp
MAX = mybir.AluOpType.max

P = 128
PACK = 4
QUADRANT = 32
SCALE_ROWS = 4
PER_COLUMN = 16
BANK = 512
HALF = 128
LAST = PACK - 1


def tile_list_ladderexp_kernel(tc, xt_words, xt_scales, w_words, w_scales, sa, sg, lo, wb_words, wb_scales,
                                  offs, offs2, offs3, offs4, out):
    nc = tc.nc
    with ExitStack() as ctx:
        sbuf = ctx.enter_context(tc.tile_pool(name="sbuf", bufs=1))
        psum = ctx.enter_context(tc.psum_pool(name="psum", bufs=1))

        def tile(name, shape, dtype):
            return sbuf.tile(shape, dtype, name=name, align_bytes=64)

        def bank(name):
            return psum.tile([P, BANK], F32, name=name)

        def entries(list_tile, first, end):
            return list_tile[:, first // PER_COLUMN : end // PER_COLUMN]

        token_list = tile("token_list", [P, J // PER_COLUMN], U16)
        put_list = tile("put_list", [P, J // PER_COLUMN], U16)
        fetch_list = tile("fetch_list", [P, C // PER_COLUMN], U16)
        place_list = tile("place_list", [P, O // PER_COLUMN], U16)
        x_words = tile("x_words", [P, T], U32)
        w_scale_rows = tile("w_scale_rows", [SCALE_ROWS, SCALE_ROWS * R], U8)
        x_plane = tile("x_plane", [P, T], U8)
        w_packed = tile("w_packed", [P, R], U16)
        w_plane = tile("w_plane", [P, R], U8)
        w_dealt = tile("w_dealt", [P, R], U16)
        w_plane_dealt = tile("w_plane_dealt", [P, R], U8)
        picked_words = tile("picked_words", [P, J], U32)
        picked_plane = tile("picked_plane", [P, J], U8)
        weight = tile("weight", [P, PACK], F32)
        slope = tile("slope", [P, PACK], F32)
        level = tile("level", [P, PACK], F32)
        wb_packed = tile("wb_packed", [P, N], U32)
        wb_plane = tile("wb_plane", [P, N], U8)
        board = [tile("board%d" % s, [P, 2 * C], F32) for s in range(LAST)]
        board.append(board[0])
        kept = [tile("kept%d" % s, [P, C], F32) for s in range(PACK)]
        fetched = [tile("fetched%d" % s, [P, C], F32) for s in range(PACK)]
        hidden = [tile("hidden%d" % s, [P, J], F32) for s in range(LAST)]
        hidden.append(kept[LAST - 1][:, 0:J])
        hid = tile("hid", [P, PACK * O], BF16)
        hid_words = tile("hid_words", [P, O], U32)
        hid_plane = tile("hid_plane", [P, O], U8)

        def load_plane(plane, scales):
            for i in range(SCALE_ROWS):
                nc.sync.dma_start(plane[i:P:QUADRANT, :].bitcast(I32), scales[0, i : SCALE_ROWS * SCALE_ROWS : SCALE_ROWS, :].bitcast(I32))

        nc.vector.memset(x_plane[:].bitcast(I32), 0)
        nc.vector.memset(w_plane[:].bitcast(I32), 0)

        nc.sync.dma_start(w_scale_rows[:].bitcast(I32).rearrange("i (q c) -> i q c", q=SCALE_ROWS),
                          w_scales[0].bitcast(I32).rearrange("(q i) c -> i q c", i=SCALE_ROWS))
        nc.sync.dma_start(token_list[:], offs)
        nc.sync.dma_start(w_packed[:].bitcast(I32), w_words[0].bitcast(I32))
        load_plane(x_plane, xt_scales)
        nc.sync.dma_start(x_words[:].bitcast(I32), xt_words[0].rearrange("p t i -> p (t i)").bitcast(I32))
        nc.sync.dma_start(put_list[:], offs2)
        nc.sync.dma_start(fetch_list[:], offs3)
        nc.sync.dma_start(weight[:], sa.rearrange("(p s) o -> p (s o)", s=PACK))
        nc.sync.dma_start(place_list[:], offs4)
        nc.sync.dma_start(slope[:], sg.rearrange("(p s) o -> p (s o)", s=PACK))
        nc.sync.dma_start(level[:], lo.rearrange("(p s) o -> p (s o)", s=PACK))
        nc.sync.dma_start(wb_packed[:].bitcast(I32), wb_words[0].rearrange("p n i -> p (n i)").bitcast(I32))

        for s in range(LAST):
            nc.vector.memset(board[s][:, 0:C], 0.0)
        nc.vector.memset(wb_plane[:].bitcast(I32), 0)
        load_plane(wb_plane, wb_scales)

        nc.scalar.copy(w_dealt[:].rearrange("p (s m) -> p s m", s=PACK), w_packed[:].rearrange("p (m s) -> p s m", s=PACK))

        for q in range(SCALE_ROWS):
            nc.vector.tensor_copy(w_plane[QUADRANT * q : QUADRANT * q + SCALE_ROWS, :].bitcast(I32),
                                  w_scale_rows[:, q * R : (q + 1) * R].bitcast(I32))
        plane_by_slice = w_plane[:].rearrange("p (m s) -> p s m", s=PACK)
        dealt_by_slice = w_plane_dealt[:].rearrange("p (s m) -> p s m", s=PACK)
        nc.vector.tensor_copy(picked_plane[:, 0:HALF], x_plane[:].indirect(entries(token_list, 0, HALF)))
        nc.vector.tensor_copy(dealt_by_slice[:, 0, :], plane_by_slice[:, 0, :])
        nc.vector.tensor_copy(picked_words[:, 0:HALF], x_words[:].indirect(entries(token_list, 0, HALF)))
        nc.vector.tensor_copy(picked_plane[:, HALF:J], x_plane[:].indirect(entries(token_list, HALF, J)))
        nc.vector.tensor_copy(picked_words[:, HALF:J], x_words[:].indirect(entries(token_list, HALF, J)))
        nc.vector.tensor_copy(dealt_by_slice[:, 1:PACK, :], plane_by_slice[:, 1:PACK, :])

        def first_product(acc, s, first, end):
            features = slice(s * P, (s + 1) * P)
            nc.tensor.matmul_mx(out=acc[:, 0 : end - first], lhsT=w_dealt[:, features].bitcast(FP4X4),
                                lhsT_scale=w_plane_dealt[:, features], rhs=picked_words[:, first:end].bitcast(FP8X4),
                                rhs_scale=picked_plane[:, first:end], start=True, stop=True)

        half_acc = [bank("half_acc%d" % h) for h in range(2)]
        slice_acc = {s: bank("slice_acc%d" % s) for s in range(1, PACK)}
        for h in range(2):
            first_product(half_acc[h], 0, h * HALF, (h + 1) * HALF)
        for s in range(1, PACK):
            first_product(slice_acc[s], s, 0, J)

        nc.scalar.copy(hidden[0][:, 0:HALF], half_acc[0][:, 0:HALF])
        nc.scalar.activation(board[0][:].indirect(entries(put_list, 0, HALF)), hidden[0][:, 0:HALF], COPY)
        nc.vector.tensor_copy(hidden[0][:, HALF:J], half_acc[1][:, 0:HALF])
        nc.scalar.activation(board[0][:].indirect(entries(put_list, HALF, J)), hidden[0][:, HALF:J], COPY)

        def drain(s):
            nc.vector.tensor_copy(hidden[s][:, 0:J], slice_acc[s][:, 0:J])

        def put(s):
            nc.vector.tensor_copy(board[s][:].indirect(put_list[:]), hidden[s][:, 0:J])

        def fetch(s, first, end):
            nc.scalar.activation(fetched[s][:, first:end], board[s][:].indirect(entries(fetch_list, first, end)),
                                 COPY, scale=weight[:, s : s + 1])

        def keep(s, first, end):
            nc.vector.tensor_tensor(kept[s][:, first:end], board[s][:, first:end], fetched[s][:, first:end], MAX)

        def look(s, first, end):
            nc.scalar.activation(hid[:, PACK * first + s : PACK * end : PACK],
                                 kept[s][:].indirect(entries(place_list, first, end)),
                                 EXP, bias=level[:, s : s + 1], scale=slope[:, s : s + 1])

        middle = range(1, LAST)
        for s in middle:
            drain(s)
        for s in middle:
            put(s)
        drain(LAST)
        for s in range(LAST):
            fetch(s, 0, C)
        for s in range(LAST - 1):
            keep(s, 0, C)
        put(LAST)
        for s in range(LAST - 1):
            look(s, 0, O)
        keep(LAST - 1, 0, C)

        for first in (0, C // 2):
            fetch(LAST, first, first + C // 2)
        for first in (0, C // 2):
            keep(LAST, first, first + C // 2)
        look(LAST - 1, 0, O)
        for first in (0, HALF):
            look(LAST, first, first + HALF)

        for first in (0, HALF):
            places = slice(first, first + HALF)
            nc.vector.quantize_mx(out=hid_words[:, places].bitcast(FP8X4), scales=hid_plane[:, places],
                                  in_=hid[:, PACK * first : PACK * (first + HALF)])

        def second_product(acc, h, places):
            rows = slice(h * P, (h + 1) * P)
            nc.tensor.matmul_mx(out=acc, lhsT=wb_packed[:, rows].bitcast(FP8X4), lhsT_scale=wb_plane[:, rows],
                                rhs=hid_words[:, places].bitcast(FP8X4), rhs_scale=hid_plane[:, places],
                                start=True, stop=True)

        early_acc = bank("early_acc")
        late_acc = [bank("late_acc%d" % h) for h in range(2)]
        for h in range(2):
            second_product(early_acc[:, h * HALF : (h + 1) * HALF], h, slice(0, HALF))
        for h in range(2):
            second_product(late_acc[h][:, 0:HALF], h, slice(HALF, O))
        early = tile("early", [P, 2 * HALF], F32)
        nc.vector.tensor_copy(early[:], early_acc[:, 0 : 2 * HALF])
        nc.sync.dma_start(out.rearrange("(h p) o -> p h o", p=P)[:, :, 0:HALF], early[:].rearrange("p (h o) -> p h o", h=2))
        late = [tile("late%d" % h, [P, HALF], F32) for h in range(2)]
        nc.vector.tensor_copy(late[0][:], late_acc[0][:, 0:HALF])
        nc.sync.dma_start(out[0:P, HALF:O], late[0][:])
        nc.scalar.copy(late[1][:], late_acc[1][:, 0:HALF])
        nc.scalar.dma_start(out[P : 2 * P, HALF:O], late[1][:])
